import numpy as np, ml_dtypes
CORES = [78,86,94,102,110,118]
N = 6
F = 256
def setup_inputs(rng):
    return {"gr": rng.standard_normal((N, 128, N * F), dtype=np.float32).astype(ml_dtypes.bfloat16)}
def setup_inputs_big(rng):
    d = setup_inputs(rng)
    for k in ("gr",): d[k] = (d[k].astype(np.float32) * 1048576.0).astype(d[k].dtype)
    return d
def setup_inputs_small(rng):
    d = setup_inputs(rng)
    for k in ("gr",): d[k] = (d[k].astype(np.float32) * (1 / 1048576.0)).astype(d[k].dtype)
    return d
def setup_inputs_apart(rng):
    d = setup_inputs(rng)
    f = (10.0 ** rng.permutation(np.linspace(-1.5, 1.5, N))).astype(np.float32).reshape(N, 1, 1)
    for k in ("gr",): d[k] = (d[k].astype(np.float32) * f).astype(d[k].dtype)
    return d
def reference(gr):
    s = gr.astype(np.float64).sum(axis=0)
    return {"y": np.stack([s[:, F * r:F * r + F] for r in range(N)]).astype(np.float32 if gr.dtype != np.float64 else np.float64)}

from concourse.mybir import AluOpType

N = 6
F = 256

SCRATCH = {
    "src": ("sbuf", [128, N * F], "bfloat16"),
    "land": ("sbuf", [128, N * F], "bfloat16"),
    "acc0": ("psum", [128, 512], "float32"),
    "acc1": ("psum", [128, 512], "float32"),
    "out": ("sbuf", [128, F], "float32"),
}
SEMAPHORES = (["ld%d" % j for j in range(N)] + ["arr%d" % j for j in range(N)] + ["sent", "vs", "stored"])


def rank_program(g, core, T, topo):
    r = T.rank_of(core)
    if r is None:
        return

    def blk(t, j):
        return t[:, j * F:(j + 1) * F]

    order = [(r + k) % N for k in range(1, N)]

    queues = [g.sync, g.scalar]
    for i, j in enumerate(order + [r]):
        queues[i % 2].dma_start(blk(T.src, j), blk(T.gr, j)).then_inc(T.sem["ld%d" % j], 16)

    sent = 0
    for j in order:
        dst = T.cores[j]
        rid, pid, _ = topo.addr(dst)
        m = topo.mask(core, dst)
        g.wait_ge(T.sem["ld%d" % j], 16)
        g.remote_dma(out_ap=blk(T.land, r), in_ap=blk(T.src, j), remote_sem=T.sem["arr%d" % r],
                     local_sem=T.sem.sent, pid=pid, routing_id=rid, dma_engine_mask=m)
        sent += bin(m).count("1")

    v = g.vector
    v.wait_ge(T.sem["ld%d" % r], 16)
    prev = blk(T.src, r)
    accs = [T.acc0, T.acc1]
    for k in range(1, N):
        s = (r - k) % N
        v.wait_ge(T.sem["arr%d" % s], bin(topo.mask(T.cores[s], core)).count("1"))
        if k > 1:
            v.wait_ge(T.sem.vs, k - 1)
        out = T.out[:] if k == N - 1 else accs[k % 2][:, 0:F]
        v.tensor_tensor(out, prev, blk(T.land, s), AluOpType.add).then_inc(T.sem.vs, 1)
        prev = out

    g.sync.wait_ge(T.sem.vs, N - 1)
    g.sync.dma_start(T.y[:], T.out[:]).then_inc(T.sem.stored, 16)
    g.sync.wait_ge(T.sem.stored, 16)
    g.wait_ge(T.sem.sent, sent)
